import numpy as np
import ml_dtypes


def mxq(x, axis, fmt="e4m3"):
    dtype, down = {"e4m3": (ml_dtypes.float8_e4m3fn, 7), "e5m2": (ml_dtypes.float8_e5m2, 14)}[fmt]
    v = np.moveaxis(np.asarray(x, np.float32).astype(ml_dtypes.bfloat16).astype(np.float64), axis, -1)
    blocks = v.reshape(v.shape[:-1] + (-1, 32))
    amax = np.abs(blocks).max(-1, keepdims=True)
    byte = np.maximum(np.where(amax > 0, np.frexp(amax)[1] - 1 + 127, 0) - down, 1)
    scale = np.exp2(byte - 127.0)
    codes = (blocks / scale).astype(np.float32).astype(dtype).astype(np.float64)
    return np.moveaxis((codes * scale).reshape(v.shape), -1, axis)


WIDE = False


def mx_kscale(k):
    if not WIDE:
        return np.ones(k)
    levels = np.array([10, -10, 5, -5, 0])
    if k % 512:
        return np.exp2(np.random.permutation(np.resize(levels, k // 32))).repeat(32)
    a = np.empty((k // 512, 16))
    for p in range(k // 512):
        a[p, :8] = np.random.permutation(np.resize(levels, 8))
        for g in range(8):
            far = levels[np.abs(levels - a[p, g]) >= 10]
            a[p, g + 8] = far[np.random.randint(len(far))]
    return np.exp2(a.ravel()).repeat(32)


def f64(x):
    return np.asarray(x).astype(np.float64)


def striped(idx):
    return np.tile(idx.reshape(-1, 16).T, (8, 1)).astype(np.uint16)


def unstriped(offs):
    return offs[:16].T.reshape(-1).astype(np.int64)


E2M1 = np.array([0.0, 0.5, 1.0, 1.5, 2.0, 3.0, 4.0, 6.0, -0.0, -0.5, -1.0, -1.5, -2.0, -3.0, -4.0, -6.0])


def pack_weight(w, fmt):
    k, n = w.shape
    w = f64(np.asarray(w, np.float32).astype(ml_dtypes.bfloat16)).reshape(k // 32, 32, n)
    amax = np.abs(w).max(1)
    if fmt == "e4m3":
        byte = np.frexp(amax)[1] - 1 + 127 - 7
    else:
        mant, ex = np.frexp(amax / 6.0)
        byte = np.where(mant > 0.5, ex, ex - 1) + 127
    byte = np.clip(np.where(amax > 0, byte, 1), 1, 254)
    scaled = (w * np.exp2(127.0 - byte)[:, None, :]).reshape(k, n).astype(np.float32)
    by_word = np.ascontiguousarray(scaled.reshape(k // 512, 128, 4, n).transpose(0, 1, 3, 2))
    if fmt == "e4m3":
        words = by_word.astype(ml_dtypes.float8_e4m3fn).view(np.uint8)
    else:
        c = by_word.astype(ml_dtypes.float4_e2m1fn).view(np.uint8) & 0xF
        words = (c[..., 0::2] | (c[..., 1::2] << 4)).reshape(k // 512, 128, 2 * n)
    return np.ascontiguousarray(words), np.ascontiguousarray(byte.astype(np.uint8).reshape(k // 512, 16, n))


def unpack_weight(words, scales, fmt):
    g, _, n = scales.shape
    words = np.ascontiguousarray(words).reshape(g, 128, n, -1)
    if fmt == "e4m3":
        vals = words.view(ml_dtypes.float8_e4m3fn).astype(np.float64)
    else:
        nib = np.empty((g, 128, n, 4), np.uint8)
        nib[..., 0::2] = words & 0xF
        nib[..., 1::2] = words >> 4
        vals = E2M1[nib]
    vals = vals * np.repeat(np.exp2(scales.astype(np.float64) - 127.0), 8, axis=1)[..., None]
    return vals.transpose(0, 1, 3, 2).reshape(g * 512, n)


K, T, E, N = 2048, 512, 2, 384
COUNTS = (128, 384)
STARTS = np.cumsum((0,) + COUNTS)
K8 = 1024


def by_expert(wq, xq):
    return np.concatenate([wq[e].T @ xq[:, STARTS[e]:STARTS[e + 1]] for e in range(E)], axis=1)


def setup_inputs():
    n = np.random.standard_normal
    s = mx_kscale(K)[:, None]
    expert = np.random.permutation(np.repeat(np.arange(E), COUNTS))
    slot_token = np.argsort(expert, kind="stable")
    w = n((E, K, N)) / np.sqrt(K) / s[None]
    w8 = [pack_weight(m[:K8], "e4m3") for m in w]
    w4 = [pack_weight(m[K8:], "e2m1") for m in w]
    return {
        "xT": (n((K, T)) * s).astype(np.float32),
        "w8_words": np.stack([m[0] for m in w8]),
        "w8_scales": np.stack([m[1] for m in w8]),
        "w4_words": np.stack([m[0] for m in w4]),
        "w4_scales": np.stack([m[1] for m in w4]),
        "gate": np.tile(np.random.uniform(0.2, 1.0, T), (N, 1)).astype(np.float32),
        "offs": striped(slot_token),
    }


def reference(xT, w8_words, w8_scales, w4_words, w4_scales, gate, offs):
    idx = unstriped(offs)
    w = np.stack([np.concatenate([unpack_weight(w8_words[e], w8_scales[e], "e4m3"), unpack_weight(w4_words[e], w4_scales[e], "e2m1")]) for e in range(E)])
    xq = mxq(f64(xT)[:, idx], 0, "e4m3")
    y = by_expert(w, xq)
    out = np.zeros((N, T))
    out[:, idx] = f64(gate) * y
    return out

@@ -1,0 +1,164 @@
+import concourse.mybir as mybir
+
+K, T, E, N = 2048, 512, 2, 384
+P = 128
+PASSES = 4
+CHUNKS = 3
+E0 = 128
+PAD = 640
+WIN = 768
+FLOPS = 2 * K * T * N
+
+F32 = mybir.dt.float32
+BF16 = mybir.dt.bfloat16
+I32 = mybir.dt.int32
+U32 = mybir.dt.uint32
+U16 = mybir.dt.uint16
+U8 = mybir.dt.uint8
+FP8X4 = mybir.dt.float8_e4m3fn_x4
+FP4X4 = mybir.dt.float4_e2m1fn_x4
+COPY = mybir.ActivationFunctionType.Copy
+MULT = mybir.AluOpType.mult
+
+PLANE = ((0, 8), (0, 12), (0, 0), (1, 0))
+HALVES = (2, 1, 1, 2)
+
+
+def tile_moe_rag_lin_none_kernel(tc, xT, w8_words, w8_scales, w4_words, w4_scales, gate, offs, out):
+    nc = tc.nc
+    with (
+        tc.tile_pool(name="held", bufs=1) as held,
+        tc.psum_pool(name="psum", bufs=1) as psum,
+    ):
+        offs_t = held.tile([P, T // 16], U16, name="offs_t")
+        nc.sync.dma_start(offs_t[:], offs)
+
+        w8_t = held.tile([P, E * 2, N], U32, name="w8_t", align_bytes=64)
+        w4_t = held.tile([P, E * 2, 2 * N], U8, name="w4_t", align_bytes=64)
+        s8_t = held.tile([P, N], U8, name="s8_t", align_bytes=64)
+        s4_t = held.tile([P, E * 2, N], U8, name="s4_t", align_bytes=64)
+        gate_t = held.tile([P, CHUNKS, T], F32, name="gate_t")
+
+        raws = [[held.tile([P, 4, T // HALVES[a]], F32, name=f"raw{a}{h}") for h in range(HALVES[a])] for a in range(PASSES)]
+        bfs = [[held.tile([P, T // 2, 4], BF16, name=f"bf{a}{h}", align_bytes=64) for h in range(2)] for a in range(PASSES)]
+        codes = [held.tile([P, WIN], U32, name=f"codes{a}", align_bytes=64) for a in range(PASSES)]
+        planes = [held.tile([P, WIN], U8, name=f"plane{s}", align_bytes=64) for s in range(2)]
+        gcodes = [held.tile([P, PAD], U32, name=f"gcodes{a}", align_bytes=64) for a in range(PASSES)]
+        gplanes = [held.tile([P, PAD], U8, name=f"gplane{s}", align_bytes=64) for s in range(2)]
+
+        for s in range(2):
+            nc.gpsimd.memset(planes[s][:].bitcast(I32), 0)
+        for a in range(PASSES):
+            nc.gpsimd.memset(codes[a][:, T:WIN], 0)
+            nc.gpsimd.memset(gcodes[a][:, T:PAD], 0)
+        for s in range(2):
+            nc.gpsimd.memset(gplanes[s][:, T:PAD], 0)
+        nc.gpsimd.memset(s8_t[:].bitcast(I32), 0)
+        nc.gpsimd.memset(s4_t[:].bitcast(I32), 0)
+
+        def load_x(a):
+            rows = xT[512 * a : 512 * (a + 1), :].rearrange("(p j) t -> p j t", j=4)
+            step = T // HALVES[a]
+            for h in range(HALVES[a]):
+                nc.sync.dma_start(raws[a][h][:], rows[:, :, step * h : step * (h + 1)])
+
+        load_x(0)
+        load_x(1)
+        load_x(2)
+        for q in range(4):
+            nc.gpsimd.dma_start(s8_t[32 * q : 32 * q + 16, :].bitcast(I32), w8_scales[:, :, 4 * q : 4 * q + 4, :].bitcast(I32).rearrange("e a q n -> (e a) q n"))
+        for q in range(4):
+            nc.gpsimd.dma_start(s4_t[32 * q : 32 * q + 4, :, :].bitcast(I32), w4_scales[:, :, 4 * q : 4 * q + 4, :].bitcast(I32).rearrange("e a q n -> q (e a) n"))
+
+        def load_w8(e):
+            nc.sync.dma_start(w8_t[:, 2 * e : 2 * e + 2, :].bitcast(I32), w8_words[e].bitcast(I32).rearrange("a p n one -> p a (n one)"))
+
+        def load_w4(e):
+            nc.sync.dma_start(w4_t[:, 2 * e : 2 * e + 2, :].bitcast(I32), w4_words[e].bitcast(I32).rearrange("a p n -> p a n"))
+
+        load_w8(1)
+        load_x(3)
+        load_w8(0)
+        load_w4(0)
+        load_w4(1)
+        for c in range(CHUNKS):
+            nc.sync.dma_start(gate_t[:, c, :], gate[128 * c : 128 * (c + 1), :])
+
+        def cast(engine, a, h, t0, t1):
+            dst = bfs[a][h][:, t0:t1, :].rearrange("p (c i) j -> p c j i", i=4)
+            raw = raws[a][h][:, :, t0:t1] if HALVES[a] == 2 else raws[a][0][:, :, 256 * h + t0 : 256 * h + t1]
+            src = raw.rearrange("p j (c i) -> p c j i", i=4)
+            if engine == "scalar":
+                nc.scalar.activation(out=dst, in_=src, func=COPY)
+            else:
+                nc.vector.tensor_copy(out=dst, in_=src)
+
+        def quantise(a, h):
+            s, k = PLANE[a]
+            nc.vector.quantize_mx(
+                out=codes[a][:, 256 * h : 256 * (h + 1)].bitcast(FP8X4),
+                scales=planes[s][k:P, 256 * h : 256 * (h + 1)],
+                in_=bfs[a][h][:].rearrange("p t j -> p (t j)"),
+            )
+
+        def gather(dst, src, j0, j1):
+            nc.vector.tensor_copy(dst[:, j0:j1], src[:].indirect(offs_t[:, j0 // 16 : j1 // 16]))
+
+        accs = [[psum.tile([P, width], F32, name=f"acc{c}{e}") for e, width in enumerate((E0, T))] for c in range(CHUNKS)]
+
+        def multiply(a, c, e):
+            s, k = PLANE[a]
+            cols = slice(0, E0) if e == 0 else slice(E0, PAD)
+            m = slice(128 * c, 128 * (c + 1))
+            if a < 2:
+                u = 2 * e + a
+                w = w8_t[:, u, m].bitcast(FP8X4)
+                ws = s8_t[4 * u : P, m]
+            else:
+                u = 2 * e + a - 2
+                w = w4_t[:, u, 256 * c : 256 * (c + 1)].bitcast(FP4X4)
+                ws = s4_t[:, u, m]
+            nc.tensor.matmul_mx(
+                out=accs[c][e][:],
+                lhsT=w,
+                lhsT_scale=ws,
+                rhs=gcodes[a][:, cols].bitcast(FP8X4),
+                rhs_scale=gplanes[s][k:P, cols],
+                start=(a == 0),
+                stop=(a == PASSES - 1),
+            )
+
+        for a in range(PASSES):
+            cast("scalar", a, 0, 0, 256)
+            if a < 3:
+                cast("scalar", a, 1, 0, 256)
+            else:
+                cast("scalar", a, 1, 0, 128)
+                cast("vector", a, 1, 128, 256)
+            quantise(a, 0)
+            quantise(a, 1)
+            if a < 3:
+                gather(gcodes[a], codes[a], 0, T)
+            if a == 2:
+                gather(gplanes[0], planes[0], 0, T)
+
+        for a, e in ((0, 1), (1, 1), (0, 0), (1, 0), (2, 0)):
+            for c in range(CHUNKS):
+                multiply(a, c, e)
+
+        ress = [held.tile([P, T], F32, name=f"res{c}") for c in range(CHUNKS)]
+        wins = [held.tile([P, WIN], F32, name=f"win{c}") for c in range(CHUNKS)]
+        for e, (j0, j1) in enumerate(((0, E0), (E0, T))):
+            gather(gcodes[3], codes[3], j0, j1)
+            gather(gplanes[1], planes[1], j0, j1)
+            if e == 1:
+                for c in range(CHUNKS):
+                    multiply(2, c, 1)
+            for c in range(CHUNKS):
+                multiply(PASSES - 1, c, e)
+                nc.scalar.activation(out=ress[c][:, j0:j1], in_=accs[c][e][:, 0 : j1 - j0], func=COPY)
+        for e, (j0, j1) in enumerate(((0, E0), (E0, T))):
+            for c in range(CHUNKS):
+                nc.vector.tensor_tensor(wins[c][:].indirect(offs_t[:, j0 // 16 : j1 // 16]), ress[c][:, j0:j1], gate_t[:, c, j0:j1], MULT)
+                if e == 1:
+                    nc.sync.dma_start(out[128 * c : 128 * (c + 1), :], wins[c][:, 0:T])

@@ -5,7 +5,6 @@ P = 128
 PASSES = 4
 CHUNKS = 3
 E0 = 128
-PAD = 640
 WIN = 768
 FLOPS = 2 * K * T * N
 
@@ -43,18 +42,13 @@ def tile_moe_rag_lin_none_kernel(tc, xT, w8_words, w8_scales, w4_words, w4_scale
         bfs = [[held.tile([P, T // 2, 4], BF16, name=f"bf{a}{h}", align_bytes=64) for h in range(2)] for a in range(PASSES)]
         codes = [held.tile([P, WIN], U32, name=f"codes{a}", align_bytes=64) for a in range(PASSES)]
         planes = [held.tile([P, WIN], U8, name=f"plane{s}", align_bytes=64) for s in range(2)]
-        gcodes = [held.tile([P, PAD], U32, name=f"gcodes{a}", align_bytes=64) for a in range(PASSES)]
-        gplanes = [held.tile([P, PAD], U8, name=f"gplane{s}", align_bytes=64) for s in range(2)]
+        gcodes = [held.tile([P, T], U32, name=f"gcodes{a}", align_bytes=64) for a in range(PASSES)]
+        gplanes = [held.tile([P, T], U8, name=f"gplane{s}", align_bytes=64) for s in range(2)]
 
+        nc.vector.memset(s8_t[:].bitcast(I32), 0)
+        nc.vector.memset(s4_t[:].bitcast(I32), 0)
         for s in range(2):
-            nc.gpsimd.memset(planes[s][:].bitcast(I32), 0)
-        for a in range(PASSES):
-            nc.gpsimd.memset(codes[a][:, T:WIN], 0)
-            nc.gpsimd.memset(gcodes[a][:, T:PAD], 0)
-        for s in range(2):
-            nc.gpsimd.memset(gplanes[s][:, T:PAD], 0)
-        nc.gpsimd.memset(s8_t[:].bitcast(I32), 0)
-        nc.gpsimd.memset(s4_t[:].bitcast(I32), 0)
+            nc.vector.memset(planes[s][:].bitcast(I32), 0)
 
         def load_x(a):
             rows = xT[512 * a : 512 * (a + 1), :].rearrange("(p j) t -> p j t", j=4)
@@ -68,7 +62,7 @@ def tile_moe_rag_lin_none_kernel(tc, xT, w8_words, w8_scales, w4_words, w4_scale
         for q in range(4):
             nc.gpsimd.dma_start(s8_t[32 * q : 32 * q + 16, :].bitcast(I32), w8_scales[:, :, 4 * q : 4 * q + 4, :].bitcast(I32).rearrange("e a q n -> (e a) q n"))
         for q in range(4):
-            nc.gpsimd.dma_start(s4_t[32 * q : 32 * q + 4, :, :].bitcast(I32), w4_scales[:, :, 4 * q : 4 * q + 4, :].bitcast(I32).rearrange("e a q n -> q (e a) n"))
+            nc.scalar.dma_start(s4_t[32 * q : 32 * q + 4, :, :].bitcast(I32), w4_scales[:, :, 4 * q : 4 * q + 4, :].bitcast(I32).rearrange("e a q n -> q (e a) n"))
 
         def load_w8(e):
             nc.sync.dma_start(w8_t[:, 2 * e : 2 * e + 2, :].bitcast(I32), w8_words[e].bitcast(I32).rearrange("a p n one -> p a (n one)"))
@@ -76,11 +70,10 @@ def tile_moe_rag_lin_none_kernel(tc, xT, w8_words, w8_scales, w4_words, w4_scale
         def load_w4(e):
             nc.sync.dma_start(w4_t[:, 2 * e : 2 * e + 2, :].bitcast(I32), w4_words[e].bitcast(I32).rearrange("a p n -> p a n"))
 
-        load_w8(1)
         load_x(3)
-        load_w8(0)
-        load_w4(0)
-        load_w4(1)
+        for e in range(E):
+            load_w8(e)
+            load_w4(e)
         for c in range(CHUNKS):
             nc.sync.dma_start(gate_t[:, c, :], gate[128 * c : 128 * (c + 1), :])
 
@@ -104,11 +97,11 @@ def tile_moe_rag_lin_none_kernel(tc, xT, w8_words, w8_scales, w4_words, w4_scale
         def gather(dst, src, j0, j1):
             nc.vector.tensor_copy(dst[:, j0:j1], src[:].indirect(offs_t[:, j0 // 16 : j1 // 16]))
 
-        accs = [[psum.tile([P, width], F32, name=f"acc{c}{e}") for e, width in enumerate((E0, T))] for c in range(CHUNKS)]
+        accs = [[psum.tile([P, width], F32, name=f"acc{c}{e}") for e, width in enumerate((E0, T - E0))] for c in range(CHUNKS)]
 
-        def multiply(a, c, e):
+        def multiply(a, c, e, b):
             s, k = PLANE[a]
-            cols = slice(0, E0) if e == 0 else slice(E0, PAD)
+            cols = slice(0, E0) if e == 0 else slice(E0 + 128 * b, E0 + 128 * (b + 1))
             m = slice(128 * c, 128 * (c + 1))
             if a < 2:
                 u = 2 * e + a
@@ -119,7 +112,7 @@ def tile_moe_rag_lin_none_kernel(tc, xT, w8_words, w8_scales, w4_words, w4_scale
                 w = w4_t[:, u, 256 * c : 256 * (c + 1)].bitcast(FP4X4)
                 ws = s4_t[:, u, m]
             nc.tensor.matmul_mx(
-                out=accs[c][e][:],
+                out=accs[c][e][:, 128 * b : 128 * (b + 1)],
                 lhsT=w,
                 lhsT_scale=ws,
                 rhs=gcodes[a][:, cols].bitcast(FP8X4),
@@ -130,7 +123,7 @@ def tile_moe_rag_lin_none_kernel(tc, xT, w8_words, w8_scales, w4_words, w4_scale
 
         for a in range(PASSES):
             cast("scalar", a, 0, 0, 256)
-            if a < 3:
+            if a == 0:
                 cast("scalar", a, 1, 0, 256)
             else:
                 cast("scalar", a, 1, 0, 128)
@@ -142,20 +135,23 @@ def tile_moe_rag_lin_none_kernel(tc, xT, w8_words, w8_scales, w4_words, w4_scale
             if a == 2:
                 gather(gplanes[0], planes[0], 0, T)
 
-        for a, e in ((0, 1), (1, 1), (0, 0), (1, 0), (2, 0)):
-            for c in range(CHUNKS):
-                multiply(a, c, e)
 
         ress = [held.tile([P, T], F32, name=f"res{c}") for c in range(CHUNKS)]
         wins = [held.tile([P, WIN], F32, name=f"win{c}") for c in range(CHUNKS)]
         for e, (j0, j1) in enumerate(((0, E0), (E0, T))):
             gather(gcodes[3], codes[3], j0, j1)
             gather(gplanes[1], planes[1], j0, j1)
-            if e == 1:
-                for c in range(CHUNKS):
-                    multiply(2, c, 1)
+            if e == 0:
+                for a in range(PASSES - 1):
+                    for c in range(CHUNKS):
+                        multiply(a, c, 0, 0)
             for c in range(CHUNKS):
-                multiply(PASSES - 1, c, e)
+                if e == 0:
+                    multiply(PASSES - 1, c, 0, 0)
+                else:
+                    for b in range(3):
+                        for a in range(PASSES):
+                            multiply(a, c, 1, b)
                 nc.scalar.activation(out=ress[c][:, j0:j1], in_=accs[c][e][:, 0 : j1 - j0], func=COPY)
         for e, (j0, j1) in enumerate(((0, E0), (E0, T))):
             for c in range(CHUNKS):

@@ -20,14 +20,16 @@ COPY = mybir.ActivationFunctionType.Copy
 MULT = mybir.AluOpType.mult
 
 PLANE = ((0, 8), (0, 12), (0, 0), (1, 0))
-HALVES = (2, 1, 1, 2)
+LOADS = (((0, 512),), ((0, 512),), ((0, 512),), ((0, 256), (256, 512)))
+SCALAR_CASTS = (((0, 256),), ((0, 256), (256, 320)), ((0, 256), (256, 320)), ((0, 224), (256, 512)))
+VECTOR_CASTS = (((256, 512),), ((320, 512),), ((320, 512),), ((224, 256),))
 
 
 def tile_moe_rag_lin_none_kernel(tc, xT, w8_words, w8_scales, w4_words, w4_scales, gate, offs, out):
     nc = tc.nc
     with (
         tc.tile_pool(name="held", bufs=1) as held,
-        tc.psum_pool(name="psum", bufs=1) as psum,
+        tc.psum_pool(name="psum", bufs=8) as psum,
     ):
         offs_t = held.tile([P, T // 16], U16, name="offs_t")
         nc.sync.dma_start(offs_t[:], offs)
@@ -38,8 +40,8 @@ def tile_moe_rag_lin_none_kernel(tc, xT, w8_words, w8_scales, w4_words, w4_scale
         s4_t = held.tile([P, E * 2, N], U8, name="s4_t", align_bytes=64)
         gate_t = held.tile([P, CHUNKS, T], F32, name="gate_t")
 
-        raws = [[held.tile([P, 4, T // HALVES[a]], F32, name=f"raw{a}{h}") for h in range(HALVES[a])] for a in range(PASSES)]
-        bfs = [[held.tile([P, T // 2, 4], BF16, name=f"bf{a}{h}", align_bytes=64) for h in range(2)] for a in range(PASSES)]
+        raws = [[held.tile([P, 4, t1 - t0], F32, name=f"raw{a}_{t0}") for t0, t1 in LOADS[a]] for a in range(PASSES)]
+        bfs = [held.tile([P, T, 4], BF16, name=f"bf{a}", align_bytes=64) for a in range(PASSES)]
         codes = [held.tile([P, WIN], U32, name=f"codes{a}", align_bytes=64) for a in range(PASSES)]
         planes = [held.tile([P, WIN], U8, name=f"plane{s}", align_bytes=64) for s in range(2)]
         gcodes = [held.tile([P, T], U32, name=f"gcodes{a}", align_bytes=64) for a in range(PASSES)]
@@ -50,15 +52,14 @@ def tile_moe_rag_lin_none_kernel(tc, xT, w8_words, w8_scales, w4_words, w4_scale
         for s in range(2):
             nc.vector.memset(planes[s][:].bitcast(I32), 0)
 
-        def load_x(a):
+        def load_x(a, h):
             rows = xT[512 * a : 512 * (a + 1), :].rearrange("(p j) t -> p j t", j=4)
-            step = T // HALVES[a]
-            for h in range(HALVES[a]):
-                nc.sync.dma_start(raws[a][h][:], rows[:, :, step * h : step * (h + 1)])
+            t0, t1 = LOADS[a][h]
+            nc.sync.dma_start(raws[a][h][:], rows[:, :, t0:t1])
 
-        load_x(0)
-        load_x(1)
-        load_x(2)
+        load_x(0, 0)
+        load_x(1, 0)
+        load_x(2, 0)
         for q in range(4):
             nc.gpsimd.dma_start(s8_t[32 * q : 32 * q + 16, :].bitcast(I32), w8_scales[:, :, 4 * q : 4 * q + 4, :].bitcast(I32).rearrange("e a q n -> (e a) q n"))
         for q in range(4):
@@ -70,38 +71,39 @@ def tile_moe_rag_lin_none_kernel(tc, xT, w8_words, w8_scales, w4_words, w4_scale
         def load_w4(e):
             nc.sync.dma_start(w4_t[:, 2 * e : 2 * e + 2, :].bitcast(I32), w4_words[e].bitcast(I32).rearrange("a p n -> p a n"))
 
-        load_x(3)
+        load_x(3, 0)
+        load_x(3, 1)
         for e in range(E):
             load_w8(e)
             load_w4(e)
         for c in range(CHUNKS):
             nc.sync.dma_start(gate_t[:, c, :], gate[128 * c : 128 * (c + 1), :])
 
-        def cast(engine, a, h, t0, t1):
-            dst = bfs[a][h][:, t0:t1, :].rearrange("p (c i) j -> p c j i", i=4)
-            raw = raws[a][h][:, :, t0:t1] if HALVES[a] == 2 else raws[a][0][:, :, 256 * h + t0 : 256 * h + t1]
-            src = raw.rearrange("p j (c i) -> p c j i", i=4)
+        def cast(engine, a, t0, t1):
+            h = max(i for i, (lo, hi) in enumerate(LOADS[a]) if lo <= t0)
+            lo = LOADS[a][h][0]
+            dst = bfs[a][:, t0:t1, :].rearrange("p (c i) j -> p c j i", i=4)
+            src = raws[a][h][:, :, t0 - lo : t1 - lo].rearrange("p j (c i) -> p c j i", i=4)
             if engine == "scalar":
                 nc.scalar.activation(out=dst, in_=src, func=COPY)
             else:
                 nc.vector.tensor_copy(out=dst, in_=src)
 
-        def quantise(a, h):
+        def quantise(a, t0, t1):
             s, k = PLANE[a]
             nc.vector.quantize_mx(
-                out=codes[a][:, 256 * h : 256 * (h + 1)].bitcast(FP8X4),
-                scales=planes[s][k:P, 256 * h : 256 * (h + 1)],
-                in_=bfs[a][h][:].rearrange("p t j -> p (t j)"),
+                out=codes[a][:, t0:t1].bitcast(FP8X4),
+                scales=planes[s][k:P, t0:t1],
+                in_=bfs[a][:, t0:t1, :].rearrange("p t j -> p (t j)"),
             )
 
         def gather(dst, src, j0, j1):
             nc.vector.tensor_copy(dst[:, j0:j1], src[:].indirect(offs_t[:, j0 // 16 : j1 // 16]))
 
-        accs = [[psum.tile([P, width], F32, name=f"acc{c}{e}") for e, width in enumerate((E0, T - E0))] for c in range(CHUNKS)]
-
-        def multiply(a, c, e, b):
+        def multiply(acc, a, c, j0):
             s, k = PLANE[a]
-            cols = slice(0, E0) if e == 0 else slice(E0 + 128 * b, E0 + 128 * (b + 1))
+            e = 0 if j0 < E0 else 1
+            cols = slice(j0, j0 + 128)
             m = slice(128 * c, 128 * (c + 1))
             if a < 2:
                 u = 2 * e + a
@@ -112,7 +114,7 @@ def tile_moe_rag_lin_none_kernel(tc, xT, w8_words, w8_scales, w4_words, w4_scale
                 w = w4_t[:, u, 256 * c : 256 * (c + 1)].bitcast(FP4X4)
                 ws = s4_t[:, u, m]
             nc.tensor.matmul_mx(
-                out=accs[c][e][:, 128 * b : 128 * (b + 1)],
+                out=acc[:],
                 lhsT=w,
                 lhsT_scale=ws,
                 rhs=gcodes[a][:, cols].bitcast(FP8X4),
@@ -122,37 +124,39 @@ def tile_moe_rag_lin_none_kernel(tc, xT, w8_words, w8_scales, w4_words, w4_scale
             )
 
         for a in range(PASSES):
-            cast("scalar", a, 0, 0, 256)
-            if a == 0:
-                cast("scalar", a, 1, 0, 256)
-            else:
-                cast("scalar", a, 1, 0, 128)
-                cast("vector", a, 1, 128, 256)
-            quantise(a, 0)
-            quantise(a, 1)
+            for t0, t1 in SCALAR_CASTS[a]:
+                cast("scalar", a, t0, t1)
+            for t0, t1 in VECTOR_CASTS[a]:
+                cast("vector", a, t0, t1)
+            quantise(a, 0, 256)
+            quantise(a, 256, 512)
             if a < 3:
                 gather(gcodes[a], codes[a], 0, T)
             if a == 2:
                 gather(gplanes[0], planes[0], 0, T)
-
+        for j0, j1 in ((0, E0), (E0, T)):
+            gather(gcodes[3], codes[3], j0, j1)
+            gather(gplanes[1], planes[1], j0, j1)
 
         ress = [held.tile([P, T], F32, name=f"res{c}") for c in range(CHUNKS)]
         wins = [held.tile([P, WIN], F32, name=f"win{c}") for c in range(CHUNKS)]
-        for e, (j0, j1) in enumerate(((0, E0), (E0, T))):
-            gather(gcodes[3], codes[3], j0, j1)
-            gather(gplanes[1], planes[1], j0, j1)
-            if e == 0:
-                for a in range(PASSES - 1):
-                    for c in range(CHUNKS):
-                        multiply(a, c, 0, 0)
+
+        def empty(acc, c, j0):
+            nc.scalar.activation(out=ress[c][:, j0 : j0 + 128], in_=acc[:], func=COPY)
+
+        firsts = [psum.tile([P, 128], F32, name="acc") for c in range(CHUNKS)]
+        for a in range(PASSES):
             for c in range(CHUNKS):
-                if e == 0:
-                    multiply(PASSES - 1, c, 0, 0)
-                else:
-                    for b in range(3):
-                        for a in range(PASSES):
-                            multiply(a, c, 1, b)
-                nc.scalar.activation(out=ress[c][:, j0:j1], in_=accs[c][e][:, 0 : j1 - j0], func=COPY)
+                multiply(firsts[c], a, c, 0)
+        for c in range(CHUNKS):
+            empty(firsts[c], c, 0)
+        for c in range(CHUNKS):
+            accs = [psum.tile([P, 128], F32, name="acc") for j0 in range(E0, T, 128)]
+            for a in range(PASSES):
+                for acc, j0 in zip(accs, range(E0, T, 128)):
+                    multiply(acc, a, c, j0)
+            for acc, j0 in zip(accs, range(E0, T, 128)):
+                empty(acc, c, j0)
         for e, (j0, j1) in enumerate(((0, E0), (E0, T))):
             for c in range(CHUNKS):
                 nc.vector.tensor_tensor(wins[c][:].indirect(offs_t[:, j0 // 16 : j1 // 16]), ress[c][:, j0:j1], gate_t[:, c, j0:j1], MULT)

@@ -20,9 +20,9 @@ COPY = mybir.ActivationFunctionType.Copy
 MULT = mybir.AluOpType.mult
 
 PLANE = ((0, 8), (0, 12), (0, 0), (1, 0))
-LOADS = (((0, 512),), ((0, 512),), ((0, 512),), ((0, 256), (256, 512)))
-SCALAR_CASTS = (((0, 256),), ((0, 256), (256, 320)), ((0, 256), (256, 320)), ((0, 224), (256, 512)))
-VECTOR_CASTS = (((256, 512),), ((320, 512),), ((320, 512),), ((224, 256),))
+LOADS = (((0, 512),),) * PASSES
+SCALAR_CASTS = (((0, 192),), ((0, 256), (256, 320)), ((0, 256), (256, 320)), ((0, 256), (256, 352)))
+VECTOR_CASTS = (((192, 512),), ((320, 512),), ((320, 512),), ((352, 512),))
 
 
 def tile_moe_rag_lin_none_kernel(tc, xT, w8_words, w8_scales, w4_words, w4_scales, gate, offs, out):
@@ -32,7 +32,6 @@ def tile_moe_rag_lin_none_kernel(tc, xT, w8_words, w8_scales, w4_words, w4_scale
         tc.psum_pool(name="psum", bufs=8) as psum,
     ):
         offs_t = held.tile([P, T // 16], U16, name="offs_t")
-        nc.sync.dma_start(offs_t[:], offs)
 
         w8_t = held.tile([P, E * 2, N], U32, name="w8_t", align_bytes=64)
         w4_t = held.tile([P, E * 2, 2 * N], U8, name="w4_t", align_bytes=64)
@@ -58,6 +57,7 @@ def tile_moe_rag_lin_none_kernel(tc, xT, w8_words, w8_scales, w4_words, w4_scale
             nc.sync.dma_start(raws[a][h][:], rows[:, :, t0:t1])
 
         load_x(0, 0)
+        nc.sync.dma_start(offs_t[:], offs)
         load_x(1, 0)
         load_x(2, 0)
         for q in range(4):
@@ -72,7 +72,6 @@ def tile_moe_rag_lin_none_kernel(tc, xT, w8_words, w8_scales, w4_words, w4_scale
             nc.sync.dma_start(w4_t[:, 2 * e : 2 * e + 2, :].bitcast(I32), w4_words[e].bitcast(I32).rearrange("a p n -> p a n"))
 
         load_x(3, 0)
-        load_x(3, 1)
         for e in range(E):
             load_w8(e)
             load_w4(e)

import concourse.mybir as mybir

K, T, E, N = 2048, 512, 2, 384
P = 128
PASSES = 4
CHUNKS = 3
E0 = 128
WIN = 768
FLOPS = 2 * K * T * N

F32 = mybir.dt.float32
BF16 = mybir.dt.bfloat16
I32 = mybir.dt.int32
U32 = mybir.dt.uint32
U16 = mybir.dt.uint16
U8 = mybir.dt.uint8
FP8X4 = mybir.dt.float8_e4m3fn_x4
FP4X4 = mybir.dt.float4_e2m1fn_x4
COPY = mybir.ActivationFunctionType.Copy
MULT = mybir.AluOpType.mult

PLANE = ((0, 8), (0, 12), (0, 0), (1, 0))
LOADS = (((0, 512),),) * PASSES
SCALAR_CASTS = (((0, 192),), ((0, 256), (256, 320)), ((0, 256), (256, 320)), ((0, 256), (256, 352)))
VECTOR_CASTS = (((192, 512),), ((320, 512),), ((320, 512),), ((352, 512),))


def tile_moe_rag_lin_none_kernel(tc, xT, w8_words, w8_scales, w4_words, w4_scales, gate, offs, out):
    nc = tc.nc
    with (
        tc.tile_pool(name="held", bufs=1) as held,
        tc.psum_pool(name="psum", bufs=8) as psum,
    ):
        offs_t = held.tile([P, T // 16], U16, name="offs_t")

        w8_t = held.tile([P, E * 2, N], U32, name="w8_t", align_bytes=64)
        w4_t = held.tile([P, E * 2, 2 * N], U8, name="w4_t", align_bytes=64)
        s8_t = held.tile([P, N], U8, name="s8_t", align_bytes=64)
        s4_t = held.tile([P, E * 2, N], U8, name="s4_t", align_bytes=64)
        gate_t = held.tile([P, CHUNKS, T], F32, name="gate_t")

        raws = [[held.tile([P, 4, t1 - t0], F32, name=f"raw{a}_{t0}") for t0, t1 in LOADS[a]] for a in range(PASSES)]
        bfs = [held.tile([P, T, 4], BF16, name=f"bf{a}", align_bytes=64) for a in range(PASSES)]
        codes = [held.tile([P, WIN], U32, name=f"codes{a}", align_bytes=64) for a in range(PASSES)]
        planes = [held.tile([P, WIN], U8, name=f"plane{s}", align_bytes=64) for s in range(2)]
        gcodes = [held.tile([P, T], U32, name=f"gcodes{a}", align_bytes=64) for a in range(PASSES)]
        gplanes = [held.tile([P, T], U8, name=f"gplane{s}", align_bytes=64) for s in range(2)]

        nc.vector.memset(s8_t[:].bitcast(I32), 0)
        nc.vector.memset(s4_t[:].bitcast(I32), 0)
        for s in range(2):
            nc.vector.memset(planes[s][:].bitcast(I32), 0)

        def load_x(a, h):
            rows = xT[512 * a : 512 * (a + 1), :].rearrange("(p j) t -> p j t", j=4)
            t0, t1 = LOADS[a][h]
            nc.sync.dma_start(raws[a][h][:], rows[:, :, t0:t1])

        load_x(0, 0)
        nc.sync.dma_start(offs_t[:], offs)
        load_x(1, 0)
        load_x(2, 0)
        for q in range(4):
            nc.gpsimd.dma_start(s8_t[32 * q : 32 * q + 16, :].bitcast(I32), w8_scales[:, :, 4 * q : 4 * q + 4, :].bitcast(I32).rearrange("e a q n -> (e a) q n"))
        for q in range(4):
            nc.scalar.dma_start(s4_t[32 * q : 32 * q + 4, :, :].bitcast(I32), w4_scales[:, :, 4 * q : 4 * q + 4, :].bitcast(I32).rearrange("e a q n -> q (e a) n"))

        def load_w8(e):
            nc.sync.dma_start(w8_t[:, 2 * e : 2 * e + 2, :].bitcast(I32), w8_words[e].bitcast(I32).rearrange("a p n one -> p a (n one)"))

        def load_w4(e):
            nc.sync.dma_start(w4_t[:, 2 * e : 2 * e + 2, :].bitcast(I32), w4_words[e].bitcast(I32).rearrange("a p n -> p a n"))

        load_x(3, 0)
        for e in range(E):
            load_w8(e)
            load_w4(e)
        for c in range(CHUNKS):
            nc.sync.dma_start(gate_t[:, c, :], gate[128 * c : 128 * (c + 1), :])

        def cast(engine, a, t0, t1):
            h = max(i for i, (lo, hi) in enumerate(LOADS[a]) if lo <= t0)
            lo = LOADS[a][h][0]
            dst = bfs[a][:, t0:t1, :].rearrange("p (c i) j -> p c j i", i=4)
            src = raws[a][h][:, :, t0 - lo : t1 - lo].rearrange("p j (c i) -> p c j i", i=4)
            if engine == "scalar":
                nc.scalar.activation(out=dst, in_=src, func=COPY)
            else:
                nc.vector.tensor_copy(out=dst, in_=src)

        def quantise(a, t0, t1):
            s, k = PLANE[a]
            nc.vector.quantize_mx(
                out=codes[a][:, t0:t1].bitcast(FP8X4),
                scales=planes[s][k:P, t0:t1],
                in_=bfs[a][:, t0:t1, :].rearrange("p t j -> p (t j)"),
            )

        def gather(dst, src, j0, j1):
            nc.vector.tensor_copy(dst[:, j0:j1], src[:].indirect(offs_t[:, j0 // 16 : j1 // 16]))

        def multiply(acc, a, c, j0):
            s, k = PLANE[a]
            e = 0 if j0 < E0 else 1
            cols = slice(j0, j0 + 128)
            m = slice(128 * c, 128 * (c + 1))
            if a < 2:
                u = 2 * e + a
                w = w8_t[:, u, m].bitcast(FP8X4)
                ws = s8_t[4 * u : P, m]
            else:
                u = 2 * e + a - 2
                w = w4_t[:, u, 256 * c : 256 * (c + 1)].bitcast(FP4X4)
                ws = s4_t[:, u, m]
            nc.tensor.matmul_mx(
                out=acc[:],
                lhsT=w,
                lhsT_scale=ws,
                rhs=gcodes[a][:, cols].bitcast(FP8X4),
                rhs_scale=gplanes[s][k:P, cols],
                start=(a == 0),
                stop=(a == PASSES - 1),
            )

        for a in range(PASSES):
            for t0, t1 in SCALAR_CASTS[a]:
                cast("scalar", a, t0, t1)
            for t0, t1 in VECTOR_CASTS[a]:
                cast("vector", a, t0, t1)
            quantise(a, 0, 256)
            quantise(a, 256, 512)
            if a < 3:
                gather(gcodes[a], codes[a], 0, T)
            if a == 2:
                gather(gplanes[0], planes[0], 0, T)
        for j0, j1 in ((0, E0), (E0, T)):
            gather(gcodes[3], codes[3], j0, j1)
            gather(gplanes[1], planes[1], j0, j1)

        ress = [held.tile([P, T], F32, name=f"res{c}") for c in range(CHUNKS)]
        wins = [held.tile([P, WIN], F32, name=f"win{c}") for c in range(CHUNKS)]

        def empty(acc, c, j0):
            nc.scalar.activation(out=ress[c][:, j0 : j0 + 128], in_=acc[:], func=COPY)

        firsts = [psum.tile([P, 128], F32, name="acc") for c in range(CHUNKS)]
        for a in range(PASSES):
            for c in range(CHUNKS):
                multiply(firsts[c], a, c, 0)
        for c in range(CHUNKS):
            empty(firsts[c], c, 0)
        for c in range(CHUNKS):
            accs = [psum.tile([P, 128], F32, name="acc") for j0 in range(E0, T, 128)]
            for a in range(PASSES):
                for acc, j0 in zip(accs, range(E0, T, 128)):
                    multiply(acc, a, c, j0)
            for acc, j0 in zip(accs, range(E0, T, 128)):
                empty(acc, c, j0)
        for e, (j0, j1) in enumerate(((0, E0), (E0, T))):
            for c in range(CHUNKS):
                nc.vector.tensor_tensor(wins[c][:].indirect(offs_t[:, j0 // 16 : j1 // 16]), ress[c][:, j0:j1], gate_t[:, c, j0:j1], MULT)
                if e == 1:
                    nc.sync.dma_start(out[128 * c : 128 * (c + 1), :], wins[c][:, 0:T])
